import numpy as np
import ml_dtypes


def mxq(x, axis, fmt="e4m3"):
    dtype, down = {"e4m3": (ml_dtypes.float8_e4m3fn, 7), "e5m2": (ml_dtypes.float8_e5m2, 14)}[fmt]
    v = np.moveaxis(np.asarray(x, np.float32).astype(ml_dtypes.bfloat16).astype(np.float64), axis, -1)
    blocks = v.reshape(v.shape[:-1] + (-1, 32))
    amax = np.abs(blocks).max(-1, keepdims=True)
    byte = np.maximum(np.where(amax > 0, np.frexp(amax)[1] - 1 + 127, 0) - down, 1)
    scale = np.exp2(byte - 127.0)
    codes = (blocks / scale).astype(np.float32).astype(dtype).astype(np.float64)
    return np.moveaxis((codes * scale).reshape(v.shape), -1, axis)


WIDE = False


def mx_kscale(k):
    if not WIDE:
        return np.ones(k)
    levels = np.array([10, -10, 5, -5, 0])
    if k % 512:
        return np.exp2(np.random.permutation(np.resize(levels, k // 32))).repeat(32)
    a = np.empty((k // 512, 16))
    for p in range(k // 512):
        a[p, :8] = np.random.permutation(np.resize(levels, 8))
        for g in range(8):
            far = levels[np.abs(levels - a[p, g]) >= 10]
            a[p, g + 8] = far[np.random.randint(len(far))]
    return np.exp2(a.ravel()).repeat(32)


def f64(x):
    return np.asarray(x).astype(np.float64)


def striped(idx):
    return np.tile(idx.reshape(-1, 16).T, (8, 1)).astype(np.uint16)


def unstriped(offs):
    return offs[:16].T.reshape(-1).astype(np.int64)


def relu(v):
    return np.maximum(v, 0.0)


K, T, D, S, V, H, N = 512, 4096, 3, 1024, 512, 1024, 128
P = 2 ** 7


def setup_inputs():
    n = np.random.standard_normal
    s = mx_kscale(K)[:, None]
    u = mx_kscale(H)
    q = np.random.permutation(S)
    return {
        "xT": (n((K, T)) * s).astype(np.float32),
        "w1": (n((K, H)) / np.sqrt(K) / s * u).astype(np.float32),
        "w2": (n((H, N)) / np.sqrt(H) / u[:, None]).astype(np.float32),
        "gate": np.tile(np.random.uniform(0.2, 1.0, (D, 1, V)) / np.sqrt(D), (1, P, 1)).astype(np.float32),
        "offs": striped(np.random.permutation(T)[:S]),
        "pos1": striped(q[:V]),
        "pos2": striped(q[V:]),
        "pos3": striped(np.random.permutation(S)[:V]),
    }


def reference(xT, w1, w2, gate, offs, pos1, pos2, pos3):
    h = relu(mxq(f64(w1), 0, "e4m3").T @ mxq(f64(xT)[:, unstriped(offs)], 0, "e4m3"))
    z = sum(f64(gate)[d, :1] * h[:, unstriped(p)] for d, p in enumerate((pos1, pos2, pos3)))
    return mxq(f64(w2), 0, "e4m3").T @ mxq(z, 0, "e4m3")

@@ -1,0 +1,196 @@
+from contextlib import ExitStack
+
+import concourse.mybir as mybir
+from concourse.masks import make_identity
+
+K, T, D, S, V, H, N = 512, 4096, 3, 1024, 512, 1024, 128
+FLOPS = 2 * K * S * H + 2 * H * V * N + (2 * D - 1) * H * V
+
+F32 = mybir.dt.float32
+BF16 = mybir.dt.bfloat16
+U32 = mybir.dt.uint32
+U16 = mybir.dt.uint16
+U8 = mybir.dt.uint8
+FP8X4 = mybir.dt.float8_e4m3fn_x4
+RELU = mybir.ActivationFunctionType.Relu
+MULT = mybir.AluOpType.mult
+
+P = 128
+PACK = 4
+HALF = 512
+W1_CHUNKS = ((0, 128), (128, 128), (256, 256), (512, 512))
+PIECE = 128
+
+
+def tile_picked_sage_relu_e_kernel(tc, xT, w1, w2, gate, offs, pos1, pos2, pos3, out):
+    nc = tc.nc
+    with ExitStack() as ctx:
+        lists = ctx.enter_context(tc.tile_pool(name="lists", bufs=1))
+        keep = ctx.enter_context(tc.tile_pool(name="keep", bufs=1))
+        hpool = ctx.enter_context(tc.tile_pool(name="hpool", bufs=3))
+        ypool = ctx.enter_context(tc.tile_pool(name="ypool", bufs=2))
+        psum = ctx.enter_context(tc.psum_pool(name="psum", bufs=2))
+
+        offs_sb = lists.tile([P, S // 16], U16, name="offs_sb")
+        pos_sb = [lists.tile([P, V // 16], U16, name=f"pos_sb{d}") for d in range(D)]
+
+        ident = keep.tile([P, P], F32, name="ident")
+        make_identity(nc, ident[:])
+
+        nc.sync.dma_start(offs_sb[:], offs)
+        w1_raw = [keep.tile([P, PACK, n], F32, name=f"w1_raw{i}") for i, (c, n) in enumerate(W1_CHUNKS)]
+        w1_view = w1.rearrange("(p j) c -> p j c", j=PACK)
+
+        def load_w1(i):
+            c, n = W1_CHUNKS[i]
+            nc.sync.dma_start(w1_raw[i][:], w1_view[:, :, c : c + n])
+
+        load_w1(0)
+        x_view = xT.rearrange("(p j) t -> p j t", j=PACK)
+        x_raw = [keep.tile([P, T], F32, name=f"x_raw{j}") for j in range(PACK)]
+        for j in range(PACK):
+            nc.sync.dma_start(x_raw[j][:], x_view[:, j, :])
+        gate_sb = [keep.tile([P, V], F32, name=f"gate_sb{d}") for d in range(D)]
+        pos_in = (pos1, pos2, pos3)
+        nc.sync.dma_start(pos_sb[0][:], pos_in[0])
+        nc.sync.dma_start(gate_sb[0][:], gate[0])
+        load_w1(1)
+        for d in (1, 2):
+            nc.sync.dma_start(pos_sb[d][:], pos_in[d])
+            nc.sync.dma_start(gate_sb[d][:], gate[d])
+        load_w1(2)
+        load_w1(3)
+        w2_raw = keep.tile([P, 2, PACK, N], F32, name="w2_raw")
+        nc.sync.dma_start(w2_raw[:], w2.rearrange("(g p j) m -> p g j m", j=PACK, p=P))
+
+        w1_codes = keep.tile([P, H], U32, name="w1_codes", align_bytes=64)
+        w1_scales = keep.tile([P, H], U8, name="w1_scales", align_bytes=64)
+        w1_grp = [keep.tile([P, n * PACK], BF16, name=f"w1_grp{i}", align_bytes=64) for i, (c, n) in enumerate(W1_CHUNKS)]
+
+        def group_w1(i):
+            nc.scalar.copy(w1_grp[i][:].rearrange("p (n j) -> p n j", j=PACK), w1_raw[i][:].rearrange("p j n -> p n j"))
+
+        def quantize_w1(i):
+            c, n = W1_CHUNKS[i]
+            nc.vector.quantize_mx(out=w1_codes[:, c : c + n].bitcast(FP8X4), scales=w1_scales[:, c : c + n], in_=w1_grp[i][:])
+
+        w2_grp = keep.tile([P, 2 * N * PACK], BF16, name="w2_grp", align_bytes=64)
+        w2_codes = keep.tile([P, 2 * N], U32, name="w2_codes", align_bytes=64)
+        w2_scales = keep.tile([P, 2 * N], U8, name="w2_scales", align_bytes=64)
+
+        x_grp = [keep.tile([P, HALF * PACK], BF16, name=f"x_grp{a}", align_bytes=64) for a in range(2)]
+        x_codes = [keep.tile([P, HALF], U32, name=f"x_codes{a}", align_bytes=64) for a in range(2)]
+        x_scales = [keep.tile([P, HALF], U8, name=f"x_scales{a}", align_bytes=64) for a in range(2)]
+        group_w1(0)
+        quantize_w1(0)
+        for j in range(PACK):
+            for a in range(2):
+                nc.vector.tensor_copy(
+                    x_grp[a][:].rearrange("p (n t) -> p n t", t=PACK)[:, :, j],
+                    x_raw[j][:].indirect(offs_sb[:, 32 * a : 32 * a + 32]),
+                )
+        for a in range(2):
+            nc.vector.quantize_mx(out=x_codes[a][:].bitcast(FP8X4), scales=x_scales[a][:], in_=x_grp[a][:])
+
+        def product(b):
+            h = hpool.tile([P, S], F32, name="h")
+            for a in range(2):
+                bank = psum.tile([P, HALF], F32, name="bank_h", bufs=3)
+                nc.tensor.matmul_mx(
+                    out=bank[:],
+                    lhsT=w1_codes[:, P * b : P * b + P].bitcast(FP8X4),
+                    lhsT_scale=w1_scales[:, P * b : P * b + P],
+                    rhs=x_codes[a][:].bitcast(FP8X4),
+                    rhs_scale=x_scales[a][:],
+                    start=True,
+                    stop=True,
+                )
+                dst = h[:, HALF * a : HALF * a + HALF]
+                if b == 0 and a == 1:
+                    nc.vector.tensor_scalar_max(dst, bank[:], 0.0)
+                else:
+                    nc.scalar.activation(dst, bank[:], RELU)
+            return h
+
+        def gather(h, d, y, lo, n):
+            nc.vector.tensor_tensor(y[:, lo : lo + n], h[:].indirect(pos_sb[d][:, lo // 16 : (lo + n) // 16]), gate_sb[d][:, lo : lo + n], MULT)
+
+        zT = [keep.tile([P, 4 * HALF], BF16, name=f"zT{g}") for g in range(2)]
+        z_grp = [keep.tile([P, V * PACK], BF16, name=f"z_grp{g}", align_bytes=64) for g in range(2)]
+        z_codes = [keep.tile([P, V], U32, name=f"z_codes{g}", align_bytes=64) for g in range(2)]
+        z_scales = [keep.tile([P, V], U8, name=f"z_scales{g}", align_bytes=64) for g in range(2)]
+
+        def sum_turns(ys, b, chunks):
+            bank = psum.tile([P, 4, P], F32, name="bank_z", bufs=3)
+            for c in chunks:
+                for d in range(D):
+                    nc.tensor.matmul(bank[:, c, :], ys[d][:, P * c : P * c + P], ident[:], start=(d == 0), stop=(d == D - 1), is_transpose=True)
+            lo, hi = chunks[0], chunks[-1] + 1
+            i0 = P * (b % 4)
+            nc.scalar.copy(zT[b // 4][:].rearrange("p (c i) -> p c i", c=4)[:, lo:hi, i0 : i0 + P], bank[:, lo:hi, :])
+
+        def turn_back(g, chunks, engine):
+            words = zT[g][:].bitcast(F32)
+            n = len(chunks)
+            bank = psum.tile([P, 2, 2, P], F32, name="bank_t", bufs=2)
+            for k, c in enumerate(chunks):
+                for u in range(2):
+                    nc.tensor.transpose(bank[:, k, u, :], words[:, 256 * c + u : 256 * c + 256 : 2], ident[:])
+            lo = 2 * P * chunks[0]
+            dst = z_grp[g][:].bitcast(F32)[:, lo : lo + 2 * P * n].rearrange("p (c v u) -> p c v u", c=n, u=2)
+            src = bank[:, 0:n].rearrange("p c u v -> p c v u")
+            if engine == "vector":
+                nc.vector.tensor_copy(dst, src)
+            else:
+                nc.scalar.copy(dst, src)
+
+        def quantize_z(g, lo, n):
+            nc.vector.quantize_mx(out=z_codes[g][:, lo : lo + n].bitcast(FP8X4), scales=z_scales[g][:, lo : lo + n], in_=z_grp[g][:, PACK * lo : PACK * (lo + n)])
+
+        h_next = product(0)
+        for i in (1, 2, 3):
+            group_w1(i)
+        nc.scalar.copy(w2_grp[:].rearrange("p (g n j) -> p g n j", g=2, j=PACK), w2_raw[:].rearrange("p g j n -> p g n j"))
+        firsts = {1: 1, 2: 2, 4: 3}
+        for b in range(8):
+            h = h_next
+            if b + 1 in firsts:
+                quantize_w1(firsts[b + 1])
+            if b < 7:
+                h_next = product(b + 1)
+            ys = [ypool.tile([P, V], F32, name=f"y{d}") for d in range(D)]
+            if b < 7:
+                for d in range(D):
+                    gather(h, d, ys[d], 0, V)
+                sum_turns(ys, b, (0, 1, 2, 3))
+            else:
+                gather(h, 0, ys[0], 0, V)
+                gather(h, 1, ys[1], 0, V)
+                for lo in range(0, V, PIECE):
+                    gather(h, 2, ys[2], lo, PIECE)
+                    sum_turns(ys, b, (lo // P,))
+            if b == 4:
+                turn_back(0, (0, 1), "scalar")
+                turn_back(0, (2, 3), "scalar")
+            if b == 5:
+                quantize_z(0, 0, V)
+                nc.vector.quantize_mx(out=w2_codes[:].bitcast(FP8X4), scales=w2_scales[:], in_=w2_grp[:])
+
+        o_sb = keep.tile([P, V], F32, name="o_sb")
+        for half in range(2):
+            bank = psum.tile([P, HALF], F32, name="bank_h", bufs=3)
+            for lo in range(256 * half, 256 * half + 256, PIECE):
+                turn_back(1, (lo // P,), "vector")
+                quantize_z(1, lo, PIECE)
+                for g in range(2):
+                    nc.tensor.matmul_mx(
+                        out=bank[:, lo - 256 * half : lo - 256 * half + PIECE],
+                        lhsT=w2_codes[:, N * g : N * g + N].bitcast(FP8X4),
+                        lhsT_scale=w2_scales[:, N * g : N * g + N],
+                        rhs=z_codes[g][:, lo : lo + PIECE].bitcast(FP8X4),
+                        rhs_scale=z_scales[g][:, lo : lo + PIECE],
+                        start=(g == 0),
+                        stop=(g == 1),
+                    )
+            nc.scalar.copy(o_sb[:, 256 * half : 256 * half + 256], bank[:, 0:256])
+            nc.sync.dma_start(out[:, 256 * half : 256 * half + 256], o_sb[:, 256 * half : 256 * half + 256])

@@ -18,8 +18,8 @@ MULT = mybir.AluOpType.mult
 P = 128
 PACK = 4
 HALF = 512
-W1_CHUNKS = ((0, 128), (128, 128), (256, 256), (512, 512))
-PIECE = 128
+W1_CHUNKS = ((0, 128), (128, 128), (256, 256), (512, 256), (768, 256))
+PIECES = ((0, 256), (256, 128), (384, 128))
 
 
 def tile_picked_sage_relu_e_kernel(tc, xT, w1, w2, gate, offs, pos1, pos2, pos3, out):
@@ -27,7 +27,7 @@ def tile_picked_sage_relu_e_kernel(tc, xT, w1, w2, gate, offs, pos1, pos2, pos3,
     with ExitStack() as ctx:
         lists = ctx.enter_context(tc.tile_pool(name="lists", bufs=1))
         keep = ctx.enter_context(tc.tile_pool(name="keep", bufs=1))
-        hpool = ctx.enter_context(tc.tile_pool(name="hpool", bufs=3))
+        hpool = ctx.enter_context(tc.tile_pool(name="hpool", bufs=4))
         ypool = ctx.enter_context(tc.tile_pool(name="ypool", bufs=2))
         psum = ctx.enter_context(tc.psum_pool(name="psum", bufs=2))
 
@@ -37,7 +37,6 @@ def tile_picked_sage_relu_e_kernel(tc, xT, w1, w2, gate, offs, pos1, pos2, pos3,
         ident = keep.tile([P, P], F32, name="ident")
         make_identity(nc, ident[:])
 
-        nc.sync.dma_start(offs_sb[:], offs)
         w1_raw = [keep.tile([P, PACK, n], F32, name=f"w1_raw{i}") for i, (c, n) in enumerate(W1_CHUNKS)]
         w1_view = w1.rearrange("(p j) c -> p j c", j=PACK)
 
@@ -45,11 +44,13 @@ def tile_picked_sage_relu_e_kernel(tc, xT, w1, w2, gate, offs, pos1, pos2, pos3,
             c, n = W1_CHUNKS[i]
             nc.sync.dma_start(w1_raw[i][:], w1_view[:, :, c : c + n])
 
-        load_w1(0)
         x_view = xT.rearrange("(p j) t -> p j t", j=PACK)
         x_raw = [keep.tile([P, T], F32, name=f"x_raw{j}") for j in range(PACK)]
         for j in range(PACK):
             nc.sync.dma_start(x_raw[j][:], x_view[:, j, :])
+            if j == 0:
+                nc.sync.dma_start(offs_sb[:], offs)
+        load_w1(0)
         gate_sb = [keep.tile([P, V], F32, name=f"gate_sb{d}") for d in range(D)]
         pos_in = (pos1, pos2, pos3)
         nc.sync.dma_start(pos_sb[0][:], pos_in[0])
@@ -60,6 +61,7 @@ def tile_picked_sage_relu_e_kernel(tc, xT, w1, w2, gate, offs, pos1, pos2, pos3,
             nc.sync.dma_start(gate_sb[d][:], gate[d])
         load_w1(2)
         load_w1(3)
+        load_w1(4)
         w2_raw = keep.tile([P, 2, PACK, N], F32, name="w2_raw")
         nc.sync.dma_start(w2_raw[:], w2.rearrange("(g p j) m -> p g j m", j=PACK, p=P))
 
@@ -82,34 +84,35 @@ def tile_picked_sage_relu_e_kernel(tc, xT, w1, w2, gate, offs, pos1, pos2, pos3,
         x_codes = [keep.tile([P, HALF], U32, name=f"x_codes{a}", align_bytes=64) for a in range(2)]
         x_scales = [keep.tile([P, HALF], U8, name=f"x_scales{a}", align_bytes=64) for a in range(2)]
         group_w1(0)
-        quantize_w1(0)
+        group_w1(1)
         for j in range(PACK):
             for a in range(2):
                 nc.vector.tensor_copy(
                     x_grp[a][:].rearrange("p (n t) -> p n t", t=PACK)[:, :, j],
                     x_raw[j][:].indirect(offs_sb[:, 32 * a : 32 * a + 32]),
                 )
+        quantize_w1(0)
         for a in range(2):
             nc.vector.quantize_mx(out=x_codes[a][:].bitcast(FP8X4), scales=x_scales[a][:], in_=x_grp[a][:])
 
         def product(b):
             h = hpool.tile([P, S], F32, name="h")
-            for a in range(2):
+            for a, lo, n in ((0, 0, 512), (1, 0, 512)):
                 bank = psum.tile([P, HALF], F32, name="bank_h", bufs=3)
                 nc.tensor.matmul_mx(
-                    out=bank[:],
+                    out=bank[:, 0:n],
                     lhsT=w1_codes[:, P * b : P * b + P].bitcast(FP8X4),
                     lhsT_scale=w1_scales[:, P * b : P * b + P],
-                    rhs=x_codes[a][:].bitcast(FP8X4),
-                    rhs_scale=x_scales[a][:],
+                    rhs=x_codes[a][:, lo : lo + n].bitcast(FP8X4),
+                    rhs_scale=x_scales[a][:, lo : lo + n],
                     start=True,
                     stop=True,
                 )
-                dst = h[:, HALF * a : HALF * a + HALF]
+                dst = h[:, HALF * a + lo : HALF * a + lo + n]
                 if b == 0 and a == 1:
-                    nc.vector.tensor_scalar_max(dst, bank[:], 0.0)
+                    nc.vector.tensor_scalar_max(dst, bank[:, 0:n], 0.0)
                 else:
-                    nc.scalar.activation(dst, bank[:], RELU)
+                    nc.scalar.activation(dst, bank[:, 0:n], RELU)
             return h
 
         def gather(h, d, y, lo, n):
@@ -120,14 +123,16 @@ def tile_picked_sage_relu_e_kernel(tc, xT, w1, w2, gate, offs, pos1, pos2, pos3,
         z_codes = [keep.tile([P, V], U32, name=f"z_codes{g}", align_bytes=64) for g in range(2)]
         z_scales = [keep.tile([P, V], U8, name=f"z_scales{g}", align_bytes=64) for g in range(2)]
 
-        def sum_turns(ys, b, chunks):
-            bank = psum.tile([P, 4, P], F32, name="bank_z", bufs=3)
-            for c in chunks:
-                for d in range(D):
-                    nc.tensor.matmul(bank[:, c, :], ys[d][:, P * c : P * c + P], ident[:], start=(d == 0), stop=(d == D - 1), is_transpose=True)
-            lo, hi = chunks[0], chunks[-1] + 1
+        def add_turn(bank, slot, ys, d, c):
+            nc.tensor.matmul(bank[:, slot, :], ys[d][:, P * c : P * c + P], ident[:], start=(d == 0), stop=(d == D - 1), is_transpose=True)
+
+        def store_sum(bank, b, c, n, engine):
             i0 = P * (b % 4)
-            nc.scalar.copy(zT[b // 4][:].rearrange("p (c i) -> p c i", c=4)[:, lo:hi, i0 : i0 + P], bank[:, lo:hi, :])
+            dst = zT[b // 4][:].rearrange("p (c i) -> p c i", c=4)[:, c : c + n, i0 : i0 + P]
+            if engine == "vector":
+                nc.vector.tensor_copy(dst, bank[:, 0:n, :])
+            else:
+                nc.scalar.copy(dst, bank[:, 0:n, :])
 
         def turn_back(g, chunks, engine):
             words = zT[g][:].bitcast(F32)
@@ -147,28 +152,52 @@ def tile_picked_sage_relu_e_kernel(tc, xT, w1, w2, gate, offs, pos1, pos2, pos3,
         def quantize_z(g, lo, n):
             nc.vector.quantize_mx(out=z_codes[g][:, lo : lo + n].bitcast(FP8X4), scales=z_scales[g][:, lo : lo + n], in_=z_grp[g][:, PACK * lo : PACK * (lo + n)])
 
-        h_next = product(0)
-        for i in (1, 2, 3):
-            group_w1(i)
-        nc.scalar.copy(w2_grp[:].rearrange("p (g n j) -> p g n j", g=2, j=PACK), w2_raw[:].rearrange("p g j n -> p g n j"))
-        firsts = {1: 1, 2: 2, 4: 3}
+        hs = [product(0)]
+        quantize_w1(1)
+        group_w1(2)
+        hs.append(product(1))
         for b in range(8):
-            h = h_next
-            if b + 1 in firsts:
-                quantize_w1(firsts[b + 1])
-            if b < 7:
-                h_next = product(b + 1)
+            h = hs[b]
             ys = [ypool.tile([P, V], F32, name=f"y{d}") for d in range(D)]
             if b < 7:
-                for d in range(D):
-                    gather(h, d, ys[d], 0, V)
-                sum_turns(ys, b, (0, 1, 2, 3))
-            else:
                 gather(h, 0, ys[0], 0, V)
+                if b > 0:
+                    if b in (2, 3):
+                        quantize_w1(b + 1)
+                    if b < 6:
+                        hs.append(product(b + 2))
                 gather(h, 1, ys[1], 0, V)
-                for lo in range(0, V, PIECE):
-                    gather(h, 2, ys[2], lo, PIECE)
-                    sum_turns(ys, b, (lo // P,))
+                if b == 0:
+                    quantize_w1(2)
+                    hs.append(product(2))
+                if b < 2:
+                    group_w1(b + 3)
+                if b == 3:
+                    nc.scalar.copy(w2_grp[:].rearrange("p (g n j) -> p g n j", g=2, j=PACK), w2_raw[:].rearrange("p g j n -> p g n j"))
+                gather(h, 2, ys[2], 0, V)
+                bank = psum.tile([P, 4, P], F32, name="bank_z", bufs=3)
+                for c in range(4):
+                    for d in range(D):
+                        add_turn(bank, c, ys, d, c)
+                store_sum(bank, b, 0, 4, "scalar")
+            else:
+                for d in range(D):
+                    gather(h, d, ys[d], 0, 256)
+                bank = psum.tile([P, 4, P], F32, name="bank_z", bufs=3)
+                for c in range(2):
+                    for d in range(D):
+                        add_turn(bank, c, ys, d, c)
+                store_sum(bank, b, 0, 2, "scalar")
+                for d in (0, 1):
+                    gather(h, d, ys[d], 256, 256)
+                banks = [psum.tile([P, 4, P], F32, name="bank_z", bufs=3) for c in (2, 3)]
+                for c in (2, 3):
+                    for d in (0, 1):
+                        add_turn(banks[c - 2], 0, ys, d, c)
+                for c, engine in ((2, "scalar"), (3, "vector")):
+                    gather(h, 2, ys[2], P * c, P)
+                    add_turn(banks[c - 2], 0, ys, 2, c)
+                    store_sum(banks[c - 2], b, c, 1, engine)
             if b == 4:
                 turn_back(0, (0, 1), "scalar")
                 turn_back(0, (2, 3), "scalar")
@@ -177,20 +206,22 @@ def tile_picked_sage_relu_e_kernel(tc, xT, w1, w2, gate, offs, pos1, pos2, pos3,
                 nc.vector.quantize_mx(out=w2_codes[:].bitcast(FP8X4), scales=w2_scales[:], in_=w2_grp[:])
 
         o_sb = keep.tile([P, V], F32, name="o_sb")
-        for half in range(2):
+        for lo, n in PIECES:
+            turn_back(1, tuple(range(lo // P, (lo + n) // P)), "vector" if lo == 256 else "scalar")
+            quantize_z(1, lo, n)
             bank = psum.tile([P, HALF], F32, name="bank_h", bufs=3)
-            for lo in range(256 * half, 256 * half + 256, PIECE):
-                turn_back(1, (lo // P,), "vector")
-                quantize_z(1, lo, PIECE)
-                for g in range(2):
-                    nc.tensor.matmul_mx(
-                        out=bank[:, lo - 256 * half : lo - 256 * half + PIECE],
-                        lhsT=w2_codes[:, N * g : N * g + N].bitcast(FP8X4),
-                        lhsT_scale=w2_scales[:, N * g : N * g + N],
-                        rhs=z_codes[g][:, lo : lo + PIECE].bitcast(FP8X4),
-                        rhs_scale=z_scales[g][:, lo : lo + PIECE],
-                        start=(g == 0),
-                        stop=(g == 1),
-                    )
-            nc.scalar.copy(o_sb[:, 256 * half : 256 * half + 256], bank[:, 0:256])
-            nc.sync.dma_start(out[:, 256 * half : 256 * half + 256], o_sb[:, 256 * half : 256 * half + 256])
+            for g in range(2):
+                nc.tensor.matmul_mx(
+                    out=bank[:, 0:n],
+                    lhsT=w2_codes[:, N * g : N * g + N].bitcast(FP8X4),
+                    lhsT_scale=w2_scales[:, N * g : N * g + N],
+                    rhs=z_codes[g][:, lo : lo + n].bitcast(FP8X4),
+                    rhs_scale=z_scales[g][:, lo : lo + n],
+                    start=(g == 0),
+                    stop=(g == 1),
+                )
+            if lo == 384:
+                nc.vector.tensor_copy(o_sb[:, lo : lo + n], bank[:, 0:n])
+            else:
+                nc.scalar.copy(o_sb[:, lo : lo + n], bank[:, 0:n])
+            nc.sync.dma_start(out[:, lo : lo + n], o_sb[:, lo : lo + n])

@@ -77,7 +77,6 @@ def tile_picked_sage_relu_e_kernel(tc, xT, w1, w2, gate, offs, pos1, pos2, pos3,
             nc.vector.quantize_mx(out=w1_codes[:, c : c + n].bitcast(FP8X4), scales=w1_scales[:, c : c + n], in_=w1_grp[i][:])
 
         w2_grp = keep.tile([P, 2 * N * PACK], BF16, name="w2_grp", align_bytes=64)
-        w2_codes = keep.tile([P, 2 * N], U32, name="w2_codes", align_bytes=64)
         w2_scales = keep.tile([P, 2 * N], U8, name="w2_scales", align_bytes=64)
 
         x_grp = [keep.tile([P, HALF * PACK], BF16, name=f"x_grp{a}", align_bytes=64) for a in range(2)]
@@ -85,12 +84,15 @@ def tile_picked_sage_relu_e_kernel(tc, xT, w1, w2, gate, offs, pos1, pos2, pos3,
         x_scales = [keep.tile([P, HALF], U8, name=f"x_scales{a}", align_bytes=64) for a in range(2)]
         group_w1(0)
         group_w1(1)
+        x_pair = keep.tile([P, 2, HALF], F32, name="x_pair")
         for j in range(PACK):
-            for a in range(2):
-                nc.vector.tensor_copy(
-                    x_grp[a][:].rearrange("p (n t) -> p n t", t=PACK)[:, :, j],
-                    x_raw[j][:].indirect(offs_sb[:, 32 * a : 32 * a + 32]),
-                )
+            for a in (1, 0):
+                picked = x_raw[j][:].indirect(offs_sb[:, 32 * a : 32 * a + 32])
+                if a == 1 and j >= 2:
+                    nc.vector.tensor_copy(x_pair[:, j - 2, :], picked)
+                else:
+                    nc.vector.tensor_copy(x_grp[a][:].rearrange("p (n t) -> p n t", t=PACK)[:, :, j], picked)
+        nc.scalar.copy(x_grp[1][:].rearrange("p (n t) -> p n t", t=PACK)[:, :, 2:4], x_pair[:].rearrange("p t n -> p n t"))
         quantize_w1(0)
         for a in range(2):
             nc.vector.quantize_mx(out=x_codes[a][:].bitcast(FP8X4), scales=x_scales[a][:], in_=x_grp[a][:])
@@ -120,7 +122,7 @@ def tile_picked_sage_relu_e_kernel(tc, xT, w1, w2, gate, offs, pos1, pos2, pos3,
 
         zT = [keep.tile([P, 4 * HALF], BF16, name=f"zT{g}") for g in range(2)]
         z_grp = [keep.tile([P, V * PACK], BF16, name=f"z_grp{g}", align_bytes=64) for g in range(2)]
-        z_codes = [keep.tile([P, V], U32, name=f"z_codes{g}", align_bytes=64) for g in range(2)]
+        z1_codes = keep.tile([P, V], U32, name="z1_codes", align_bytes=64)
         z_scales = [keep.tile([P, V], U8, name=f"z_scales{g}", align_bytes=64) for g in range(2)]
 
         def add_turn(bank, slot, ys, d, c):
@@ -149,8 +151,8 @@ def tile_picked_sage_relu_e_kernel(tc, xT, w1, w2, gate, offs, pos1, pos2, pos3,
             else:
                 nc.scalar.copy(dst, src)
 
-        def quantize_z(g, lo, n):
-            nc.vector.quantize_mx(out=z_codes[g][:, lo : lo + n].bitcast(FP8X4), scales=z_scales[g][:, lo : lo + n], in_=z_grp[g][:, PACK * lo : PACK * (lo + n)])
+        def quantize_z(g, codes, lo, n):
+            nc.vector.quantize_mx(out=codes[:, lo : lo + n].bitcast(FP8X4), scales=z_scales[g][:, lo : lo + n], in_=z_grp[g][:, PACK * lo : PACK * (lo + n)])
 
         hs = [product(0)]
         quantize_w1(1)
@@ -158,7 +160,7 @@ def tile_picked_sage_relu_e_kernel(tc, xT, w1, w2, gate, offs, pos1, pos2, pos3,
         hs.append(product(1))
         for b in range(8):
             h = hs[b]
-            ys = [ypool.tile([P, V], F32, name=f"y{d}") for d in range(D)]
+            ys = [ypool.tile([P, V], F32, name=f"y{d}", align_bytes=64) for d in range(D)]
             if b < 7:
                 gather(h, 0, ys[0], 0, V)
                 if b > 0:
@@ -194,28 +196,29 @@ def tile_picked_sage_relu_e_kernel(tc, xT, w1, w2, gate, offs, pos1, pos2, pos3,
                 for c in (2, 3):
                     for d in (0, 1):
                         add_turn(banks[c - 2], 0, ys, d, c)
-                for c, engine in ((2, "scalar"), (3, "vector")):
+                for c, engine in ((2, "scalar"), (3, "scalar")):
                     gather(h, 2, ys[2], P * c, P)
                     add_turn(banks[c - 2], 0, ys, 2, c)
                     store_sum(banks[c - 2], b, c, 1, engine)
+                w2_codes = ypool.tile([P, 2 * N], U32, name="w2_codes", tag="y2", align_bytes=64)
+                late = ypool.tile([P, V], U32, name="late", tag="y2", align_bytes=64)
+                nc.vector.quantize_mx(out=w2_codes[:].bitcast(FP8X4), scales=w2_scales[:], in_=w2_grp[:])
+                quantize_z(0, late, 0, V)
             if b == 4:
                 turn_back(0, (0, 1), "scalar")
                 turn_back(0, (2, 3), "scalar")
-            if b == 5:
-                quantize_z(0, 0, V)
-                nc.vector.quantize_mx(out=w2_codes[:].bitcast(FP8X4), scales=w2_scales[:], in_=w2_grp[:])
 
         o_sb = keep.tile([P, V], F32, name="o_sb")
         for lo, n in PIECES:
-            turn_back(1, tuple(range(lo // P, (lo + n) // P)), "vector" if lo == 256 else "scalar")
-            quantize_z(1, lo, n)
+            turn_back(1, tuple(range(lo // P, (lo + n) // P)), "vector" if lo == 0 else "scalar")
+            quantize_z(1, z1_codes, lo, n)
             bank = psum.tile([P, HALF], F32, name="bank_h", bufs=3)
             for g in range(2):
                 nc.tensor.matmul_mx(
                     out=bank[:, 0:n],
                     lhsT=w2_codes[:, N * g : N * g + N].bitcast(FP8X4),
                     lhsT_scale=w2_scales[:, N * g : N * g + N],
-                    rhs=z_codes[g][:, lo : lo + n].bitcast(FP8X4),
+                    rhs=(late, z1_codes)[g][:, lo : lo + n].bitcast(FP8X4),
                     rhs_scale=z_scales[g][:, lo : lo + n],
                     start=(g == 0),
                     stop=(g == 1),

@@ -99,7 +99,7 @@ def tile_picked_sage_relu_e_kernel(tc, xT, w1, w2, gate, offs, pos1, pos2, pos3,
 
         def product(b):
             h = hpool.tile([P, S], F32, name="h")
-            for a, lo, n in ((0, 0, 512), (1, 0, 512)):
+            for a, lo, n in ((0, 0, 512), (1, 0, 256), (1, 256, 256)) if b == 0 else ((0, 0, 512), (1, 0, 512)):
                 bank = psum.tile([P, HALF], F32, name="bank_h", bufs=3)
                 nc.tensor.matmul_mx(
                     out=bank[:, 0:n],
@@ -111,7 +111,7 @@ def tile_picked_sage_relu_e_kernel(tc, xT, w1, w2, gate, offs, pos1, pos2, pos3,
                     stop=True,
                 )
                 dst = h[:, HALF * a + lo : HALF * a + lo + n]
-                if b == 0 and a == 1:
+                if b == 0 and a == 1 and lo == 0:
                     nc.vector.tensor_scalar_max(dst, bank[:, 0:n], 0.0)
                 else:
                     nc.scalar.activation(dst, bank[:, 0:n], RELU)
@@ -122,7 +122,6 @@ def tile_picked_sage_relu_e_kernel(tc, xT, w1, w2, gate, offs, pos1, pos2, pos3,
 
         zT = [keep.tile([P, 4 * HALF], BF16, name=f"zT{g}") for g in range(2)]
         z_grp = [keep.tile([P, V * PACK], BF16, name=f"z_grp{g}", align_bytes=64) for g in range(2)]
-        z1_codes = keep.tile([P, V], U32, name="z1_codes", align_bytes=64)
         z_scales = [keep.tile([P, V], U8, name=f"z_scales{g}", align_bytes=64) for g in range(2)]
 
         def add_turn(bank, slot, ys, d, c):
@@ -200,9 +199,9 @@ def tile_picked_sage_relu_e_kernel(tc, xT, w1, w2, gate, offs, pos1, pos2, pos3,
                     gather(h, 2, ys[2], P * c, P)
                     add_turn(banks[c - 2], 0, ys, 2, c)
                     store_sum(banks[c - 2], b, c, 1, engine)
-                w2_codes = ypool.tile([P, 2 * N], U32, name="w2_codes", tag="y2", align_bytes=64)
-                late = ypool.tile([P, V], U32, name="late", tag="y2", align_bytes=64)
-                nc.vector.quantize_mx(out=w2_codes[:].bitcast(FP8X4), scales=w2_scales[:], in_=w2_grp[:])
+                z1_codes = ypool.tile([P, V], U32, name="z1_codes", tag="y2", align_bytes=64)
+                late = ypool.tile([P, V + 2 * N], U32, name="late", tag="y2", align_bytes=64)
+                nc.vector.quantize_mx(out=late[:, V : V + 2 * N].bitcast(FP8X4), scales=w2_scales[:], in_=w2_grp[:])
                 quantize_z(0, late, 0, V)
             if b == 4:
                 turn_back(0, (0, 1), "scalar")
@@ -216,7 +215,7 @@ def tile_picked_sage_relu_e_kernel(tc, xT, w1, w2, gate, offs, pos1, pos2, pos3,
             for g in range(2):
                 nc.tensor.matmul_mx(
                     out=bank[:, 0:n],
-                    lhsT=w2_codes[:, N * g : N * g + N].bitcast(FP8X4),
+                    lhsT=late[:, V + N * g : V + N * g + N].bitcast(FP8X4),
                     lhsT_scale=w2_scales[:, N * g : N * g + N],
                     rhs=(late, z1_codes)[g][:, lo : lo + n].bitcast(FP8X4),
                     rhs_scale=z_scales[g][:, lo : lo + n],

from contextlib import ExitStack

import concourse.mybir as mybir
from concourse.masks import make_identity

K, T, D, S, V, H, N = 512, 4096, 3, 1024, 512, 1024, 128
FLOPS = 2 * K * S * H + 2 * H * V * N + (2 * D - 1) * H * V

F32 = mybir.dt.float32
BF16 = mybir.dt.bfloat16
U32 = mybir.dt.uint32
U16 = mybir.dt.uint16
U8 = mybir.dt.uint8
FP8X4 = mybir.dt.float8_e4m3fn_x4
RELU = mybir.ActivationFunctionType.Relu
MULT = mybir.AluOpType.mult

P = 128
PACK = 4
HALF = 512
W1_CHUNKS = ((0, 128), (128, 128), (256, 256), (512, 256), (768, 256))
PIECES = ((0, 256), (256, 128), (384, 128))


def tile_picked_sage_relu_e_kernel(tc, xT, w1, w2, gate, offs, pos1, pos2, pos3, out):
    nc = tc.nc
    with ExitStack() as ctx:
        lists = ctx.enter_context(tc.tile_pool(name="lists", bufs=1))
        keep = ctx.enter_context(tc.tile_pool(name="keep", bufs=1))
        hpool = ctx.enter_context(tc.tile_pool(name="hpool", bufs=4))
        ypool = ctx.enter_context(tc.tile_pool(name="ypool", bufs=2))
        psum = ctx.enter_context(tc.psum_pool(name="psum", bufs=2))

        offs_sb = lists.tile([P, S // 16], U16, name="offs_sb")
        pos_sb = [lists.tile([P, V // 16], U16, name=f"pos_sb{d}") for d in range(D)]

        ident = keep.tile([P, P], F32, name="ident")
        make_identity(nc, ident[:])

        w1_raw = [keep.tile([P, PACK, n], F32, name=f"w1_raw{i}") for i, (c, n) in enumerate(W1_CHUNKS)]
        w1_view = w1.rearrange("(p j) c -> p j c", j=PACK)

        def load_w1(i):
            c, n = W1_CHUNKS[i]
            nc.sync.dma_start(w1_raw[i][:], w1_view[:, :, c : c + n])

        x_view = xT.rearrange("(p j) t -> p j t", j=PACK)
        x_raw = [keep.tile([P, T], F32, name=f"x_raw{j}") for j in range(PACK)]
        for j in range(PACK):
            nc.sync.dma_start(x_raw[j][:], x_view[:, j, :])
            if j == 0:
                nc.sync.dma_start(offs_sb[:], offs)
        load_w1(0)
        gate_sb = [keep.tile([P, V], F32, name=f"gate_sb{d}") for d in range(D)]
        pos_in = (pos1, pos2, pos3)
        nc.sync.dma_start(pos_sb[0][:], pos_in[0])
        nc.sync.dma_start(gate_sb[0][:], gate[0])
        load_w1(1)
        for d in (1, 2):
            nc.sync.dma_start(pos_sb[d][:], pos_in[d])
            nc.sync.dma_start(gate_sb[d][:], gate[d])
        load_w1(2)
        load_w1(3)
        load_w1(4)
        w2_raw = keep.tile([P, 2, PACK, N], F32, name="w2_raw")
        nc.sync.dma_start(w2_raw[:], w2.rearrange("(g p j) m -> p g j m", j=PACK, p=P))

        w1_codes = keep.tile([P, H], U32, name="w1_codes", align_bytes=64)
        w1_scales = keep.tile([P, H], U8, name="w1_scales", align_bytes=64)
        w1_grp = [keep.tile([P, n * PACK], BF16, name=f"w1_grp{i}", align_bytes=64) for i, (c, n) in enumerate(W1_CHUNKS)]

        def group_w1(i):
            nc.scalar.copy(w1_grp[i][:].rearrange("p (n j) -> p n j", j=PACK), w1_raw[i][:].rearrange("p j n -> p n j"))

        def quantize_w1(i):
            c, n = W1_CHUNKS[i]
            nc.vector.quantize_mx(out=w1_codes[:, c : c + n].bitcast(FP8X4), scales=w1_scales[:, c : c + n], in_=w1_grp[i][:])

        w2_grp = keep.tile([P, 2 * N * PACK], BF16, name="w2_grp", align_bytes=64)
        w2_scales = keep.tile([P, 2 * N], U8, name="w2_scales", align_bytes=64)

        x_grp = [keep.tile([P, HALF * PACK], BF16, name=f"x_grp{a}", align_bytes=64) for a in range(2)]
        x_codes = [keep.tile([P, HALF], U32, name=f"x_codes{a}", align_bytes=64) for a in range(2)]
        x_scales = [keep.tile([P, HALF], U8, name=f"x_scales{a}", align_bytes=64) for a in range(2)]
        group_w1(0)
        group_w1(1)
        x_pair = keep.tile([P, 2, HALF], F32, name="x_pair")
        for j in range(PACK):
            for a in (1, 0):
                picked = x_raw[j][:].indirect(offs_sb[:, 32 * a : 32 * a + 32])
                if a == 1 and j >= 2:
                    nc.vector.tensor_copy(x_pair[:, j - 2, :], picked)
                else:
                    nc.vector.tensor_copy(x_grp[a][:].rearrange("p (n t) -> p n t", t=PACK)[:, :, j], picked)
        nc.scalar.copy(x_grp[1][:].rearrange("p (n t) -> p n t", t=PACK)[:, :, 2:4], x_pair[:].rearrange("p t n -> p n t"))
        quantize_w1(0)
        for a in range(2):
            nc.vector.quantize_mx(out=x_codes[a][:].bitcast(FP8X4), scales=x_scales[a][:], in_=x_grp[a][:])

        def product(b):
            h = hpool.tile([P, S], F32, name="h")
            for a, lo, n in ((0, 0, 512), (1, 0, 256), (1, 256, 256)) if b == 0 else ((0, 0, 512), (1, 0, 512)):
                bank = psum.tile([P, HALF], F32, name="bank_h", bufs=3)
                nc.tensor.matmul_mx(
                    out=bank[:, 0:n],
                    lhsT=w1_codes[:, P * b : P * b + P].bitcast(FP8X4),
                    lhsT_scale=w1_scales[:, P * b : P * b + P],
                    rhs=x_codes[a][:, lo : lo + n].bitcast(FP8X4),
                    rhs_scale=x_scales[a][:, lo : lo + n],
                    start=True,
                    stop=True,
                )
                dst = h[:, HALF * a + lo : HALF * a + lo + n]
                if b == 0 and a == 1 and lo == 0:
                    nc.vector.tensor_scalar_max(dst, bank[:, 0:n], 0.0)
                else:
                    nc.scalar.activation(dst, bank[:, 0:n], RELU)
            return h

        def gather(h, d, y, lo, n):
            nc.vector.tensor_tensor(y[:, lo : lo + n], h[:].indirect(pos_sb[d][:, lo // 16 : (lo + n) // 16]), gate_sb[d][:, lo : lo + n], MULT)

        zT = [keep.tile([P, 4 * HALF], BF16, name=f"zT{g}") for g in range(2)]
        z_grp = [keep.tile([P, V * PACK], BF16, name=f"z_grp{g}", align_bytes=64) for g in range(2)]
        z_scales = [keep.tile([P, V], U8, name=f"z_scales{g}", align_bytes=64) for g in range(2)]

        def add_turn(bank, slot, ys, d, c):
            nc.tensor.matmul(bank[:, slot, :], ys[d][:, P * c : P * c + P], ident[:], start=(d == 0), stop=(d == D - 1), is_transpose=True)

        def store_sum(bank, b, c, n, engine):
            i0 = P * (b % 4)
            dst = zT[b // 4][:].rearrange("p (c i) -> p c i", c=4)[:, c : c + n, i0 : i0 + P]
            if engine == "vector":
                nc.vector.tensor_copy(dst, bank[:, 0:n, :])
            else:
                nc.scalar.copy(dst, bank[:, 0:n, :])

        def turn_back(g, chunks, engine):
            words = zT[g][:].bitcast(F32)
            n = len(chunks)
            bank = psum.tile([P, 2, 2, P], F32, name="bank_t", bufs=2)
            for k, c in enumerate(chunks):
                for u in range(2):
                    nc.tensor.transpose(bank[:, k, u, :], words[:, 256 * c + u : 256 * c + 256 : 2], ident[:])
            lo = 2 * P * chunks[0]
            dst = z_grp[g][:].bitcast(F32)[:, lo : lo + 2 * P * n].rearrange("p (c v u) -> p c v u", c=n, u=2)
            src = bank[:, 0:n].rearrange("p c u v -> p c v u")
            if engine == "vector":
                nc.vector.tensor_copy(dst, src)
            else:
                nc.scalar.copy(dst, src)

        def quantize_z(g, codes, lo, n):
            nc.vector.quantize_mx(out=codes[:, lo : lo + n].bitcast(FP8X4), scales=z_scales[g][:, lo : lo + n], in_=z_grp[g][:, PACK * lo : PACK * (lo + n)])

        hs = [product(0)]
        quantize_w1(1)
        group_w1(2)
        hs.append(product(1))
        for b in range(8):
            h = hs[b]
            ys = [ypool.tile([P, V], F32, name=f"y{d}", align_bytes=64) for d in range(D)]
            if b < 7:
                gather(h, 0, ys[0], 0, V)
                if b > 0:
                    if b in (2, 3):
                        quantize_w1(b + 1)
                    if b < 6:
                        hs.append(product(b + 2))
                gather(h, 1, ys[1], 0, V)
                if b == 0:
                    quantize_w1(2)
                    hs.append(product(2))
                if b < 2:
                    group_w1(b + 3)
                if b == 3:
                    nc.scalar.copy(w2_grp[:].rearrange("p (g n j) -> p g n j", g=2, j=PACK), w2_raw[:].rearrange("p g j n -> p g n j"))
                gather(h, 2, ys[2], 0, V)
                bank = psum.tile([P, 4, P], F32, name="bank_z", bufs=3)
                for c in range(4):
                    for d in range(D):
                        add_turn(bank, c, ys, d, c)
                store_sum(bank, b, 0, 4, "scalar")
            else:
                for d in range(D):
                    gather(h, d, ys[d], 0, 256)
                bank = psum.tile([P, 4, P], F32, name="bank_z", bufs=3)
                for c in range(2):
                    for d in range(D):
                        add_turn(bank, c, ys, d, c)
                store_sum(bank, b, 0, 2, "scalar")
                for d in (0, 1):
                    gather(h, d, ys[d], 256, 256)
                banks = [psum.tile([P, 4, P], F32, name="bank_z", bufs=3) for c in (2, 3)]
                for c in (2, 3):
                    for d in (0, 1):
                        add_turn(banks[c - 2], 0, ys, d, c)
                for c, engine in ((2, "scalar"), (3, "scalar")):
                    gather(h, 2, ys[2], P * c, P)
                    add_turn(banks[c - 2], 0, ys, 2, c)
                    store_sum(banks[c - 2], b, c, 1, engine)
                z1_codes = ypool.tile([P, V], U32, name="z1_codes", tag="y2", align_bytes=64)
                late = ypool.tile([P, V + 2 * N], U32, name="late", tag="y2", align_bytes=64)
                nc.vector.quantize_mx(out=late[:, V : V + 2 * N].bitcast(FP8X4), scales=w2_scales[:], in_=w2_grp[:])
                quantize_z(0, late, 0, V)
            if b == 4:
                turn_back(0, (0, 1), "scalar")
                turn_back(0, (2, 3), "scalar")

        o_sb = keep.tile([P, V], F32, name="o_sb")
        for lo, n in PIECES:
            turn_back(1, tuple(range(lo // P, (lo + n) // P)), "vector" if lo == 0 else "scalar")
            quantize_z(1, z1_codes, lo, n)
            bank = psum.tile([P, HALF], F32, name="bank_h", bufs=3)
            for g in range(2):
                nc.tensor.matmul_mx(
                    out=bank[:, 0:n],
                    lhsT=late[:, V + N * g : V + N * g + N].bitcast(FP8X4),
                    lhsT_scale=w2_scales[:, N * g : N * g + N],
                    rhs=(late, z1_codes)[g][:, lo : lo + n].bitcast(FP8X4),
                    rhs_scale=z_scales[g][:, lo : lo + n],
                    start=(g == 0),
                    stop=(g == 1),
                )
            if lo == 384:
                nc.vector.tensor_copy(o_sb[:, lo : lo + n], bank[:, 0:n])
            else:
                nc.scalar.copy(o_sb[:, lo : lo + n], bank[:, 0:n])
            nc.sync.dma_start(out[:, lo : lo + n], o_sb[:, lo : lo + n])
